import numpy as np
CORES = [3,7,11,15,131,135,139,143]
N = 8
KT, FB, TK = 1, 64, 512
def setup_inputs(rng):
    return {"x": rng.standard_normal((N, 128, KT * TK), dtype=np.float32), "w": rng.standard_normal((N, 128, KT * N * FB), dtype=np.float32)}
def setup_inputs_big(rng):
    d = setup_inputs(rng)
    for k in ("x", "w"): d[k] = (d[k].astype(np.float32) * 1024.0).astype(d[k].dtype)
    return d
def setup_inputs_small(rng):
    d = setup_inputs(rng)
    for k in ("x", "w"): d[k] = (d[k].astype(np.float32) * (1 / 1024.0)).astype(d[k].dtype)
    return d
def setup_inputs_apart(rng):
    d = setup_inputs(rng)
    f = (10.0 ** rng.permutation(np.linspace(-1.5, 1.5, N))).astype(np.float32).reshape(N, 1, 1)
    for k in ("x", "w"): d[k] = (d[k].astype(np.float32) * f).astype(d[k].dtype)
    return d
def reference(x, w):
    X, W = x.astype(np.float64), w.astype(np.float64)
    y = np.zeros((N, FB, N * TK))
    for j in range(N):
        for r in range(N):
            for t in range(KT):
                y[r][:, TK * j:TK * j + TK] += W[j][:, FB * (N * t + r):FB * (N * t + r) + FB].T @ X[j][:, TK * t:TK * t + TK]
    return {"y": y.astype(np.float32 if x.dtype != np.float64 else np.float64)}

@@ -1,0 +1,152 @@
+from concourse.bass import DstId, RemoteDMATransfer
+
+N, FB, TK = 8, 64, 512
+HALF = TK // 2
+
+SCRATCH = {
+    "xs": ("sbuf", [128, TK], "float32"),
+    "ws": ("sbuf", [128, N * FB], "float32"),
+    "snd": ("sbuf", [128, N * HALF], "float32"),
+    "land": ("sbuf", [128, N * HALF], "float32"),
+    "ps": ("psum", [128, 8 * TK], "float32"),
+}
+SEMAPHORES = (["ldx0", "ldx1", "ldw0", "ldw1", "ldw2", "sent", "sta", "stb"]
+              + ["mm%d" % i for i in range(8)] + ["cp%d" % i for i in range(4)] + ["arr%d" % i for i in range(N)])
+
+FAR, PLANE, MATE, OWN = 0, 1, 2, 3
+
+
+def _klass(topo, a, b):
+    if topo.host(a) == topo.host(b) and topo.chip(a) == topo.chip(b):
+        return OWN
+    if topo.mates(a, b):
+        return MATE
+    if topo.same_plane(a, b):
+        return PLANE
+    return FAR
+
+
+def _bits(mask):
+    return [b for b in range(mask.bit_length()) if (mask >> b) & 1]
+
+
+def _mask(bits):
+    m = 0
+    for b in bits:
+        m |= 1 << b
+    return m
+
+
+def _plan(topo, cores, j):
+    src = cores[j]
+    groups = {}
+    for r, c in enumerate(cores):
+        groups.setdefault((topo.host(c), topo.chip(c)), []).append(r)
+    order = sorted(groups.values(), key=lambda gr: _klass(topo, src, cores[gr[0]]))
+    kl = [_klass(topo, src, cores[gr[0]]) for gr in order]
+    calls, away = [], 0
+    for wanted in ((FAR,), (PLANE, MATE), (OWN,)):
+        steps = [i for i in range(len(order)) if kl[i] in wanted]
+        width = max(len(order[i]) for i in steps)
+        dests = [order[i][u] for u in range(width) for i in steps if u < len(order[i]) and order[i][u] != j]
+        if not dests:
+            continue
+        common = topo.mask(src, cores[dests[0]])
+        for r in dests:
+            common &= topo.mask(src, cores[r])
+        if OWN in wanted:
+            if common & ~away:
+                common &= ~away
+        else:
+            away |= common
+        bits = _bits(common)
+        calls.append((steps, [(r, _mask(bits[n::len(dests)])) for n, r in enumerate(dests)]))
+    return order, calls
+
+
+def rank_program(g, core, T, topo):
+    j = T.rank_of(core)
+    if j is None:
+        return
+    cores = list(T.cores)
+    sem = T.sem
+    order, calls = _plan(topo, cores, j)
+
+    def cols(gr):
+        return FB * gr[0], FB * (gr[-1] + 1)
+
+    lo, hi = cols(order[0])
+    ranges = [(lo, hi)] + sorted(
+        [rg for rg in ((0, lo), (hi, N * FB)) if rg[0] < rg[1]],
+        key=lambda rg: min(i for i, gr in enumerate(order) if rg[0] <= FB * gr[0] < rg[1]))
+    g.sync.dma_start(T.xs[:, 0:HALF], T.x[:, 0:HALF]).then_inc(sem.ldx0, 16)
+    g.sync.dma_start(T.xs[:, HALF:TK], T.x[:, HALF:TK]).then_inc(sem.ldx1, 16)
+    for n, (a, b) in enumerate(ranges):
+        g.scalar.dma_start(T.ws[:, a:b], T.w[:, a:b]).then_inc(sem["ldw%d" % n], 16)
+
+    seen = set()
+
+    def wait_once(q, done, name, val):
+        if name not in done:
+            done.add(name)
+            q.wait_ge(sem[name], val)
+
+    for i, gr in enumerate(order):
+        a, b = cols(gr)
+        n = [k for k, rg in enumerate(ranges) if rg[0] <= a < rg[1]][0]
+        wait_once(g.tensor, seen, "ldw%d" % n, 16)
+        for h in (0, 1):
+            wait_once(g.tensor, seen, "ldx%d" % h, 16)
+            bank = TK * (2 * i + h)
+            g.tensor.matmul(T.ps[:, bank:bank + HALF], T.ws[:, a:b], T.xs[:, HALF * h:HALF * (h + 1)],
+                            start=True, stop=True).then_inc(sem["mm%d" % (2 * i + h)], 1)
+
+    for i, gr in enumerate(order):
+        for h in (0, 1):
+            g.vector.wait_ge(sem["mm%d" % (2 * i + h)], 1)
+            bank = TK * (2 * i + h)
+            p = 0 if h == j % 2 else FB
+            for u, r in enumerate(gr):
+                out = T.land[p:p + FB, HALF * j:HALF * (j + 1)] if r == j else T.snd[p:p + FB, HALF * r:HALF * (r + 1)]
+                g.vector.tensor_copy(out, T.ps[FB * u:FB * (u + 1), bank:bank + HALF]).then_inc(sem["cp%d" % i], 1)
+    copies = [2 * len(gr) for gr in order]
+
+    total = 0
+    for steps, sends in calls:
+        for i in steps:
+            g.wait_ge(sem["cp%d" % i], copies[i])
+        trs = []
+        for r, m in sends:
+            rid, pid = topo.addr(cores[r], core)
+            trs.append(RemoteDMATransfer(dst_ids=[DstId(rid=rid, pnc=pid)], dma_engine_mask=m, remote_sem=sem["arr%d" % j],
+                                         src=T.snd[:, HALF * r:HALF * (r + 1)], dst=T.land[:, HALF * j:HALF * (j + 1)]))
+            total += len(_bits(m))
+        g.remote_dma_fused(trs, local_sem=sem.sent)
+
+    stores = []
+    for top in (True, False):
+        run = None
+        for s in range(N):
+            y0 = TK * s + HALF * (s % 2 if top else 1 - s % 2)
+            if run is not None and run[2] + HALF * len(run[1]) == y0:
+                run[1].append(s)
+            else:
+                run = [0 if top else FB, [s], y0]
+                stores.append(run)
+    own_step = [i for i, gr in enumerate(order) if j in gr][0]
+    late = {FAR: 0, OWN: 1, MATE: 2, PLANE: 3}
+    stores.sort(key=lambda st: max(late[_klass(topo, cores[s], core)] for s in st[1]))
+    queues = ((g.sync, "sta", set(), [0]), (g.scalar, "stb", set(), [0]))
+    for n, (p, ss, y0) in enumerate(stores):
+        q, name, done, count = queues[n % 2]
+        for s in ss:
+            if s == j:
+                wait_once(q, done, "cp%d" % own_step, copies[own_step])
+            else:
+                m = [m for _, sends in _plan(topo, cores, s)[1] for r, m in sends if r == j][0]
+                wait_once(q, done, "arr%d" % s, len(_bits(m)))
+        q.dma_start(T.y[:, y0:y0 + HALF * len(ss)], T.land[p:p + FB, HALF * ss[0]:HALF * (ss[-1] + 1)]).then_inc(sem[name], 16)
+        count[0] += 16
+    for q, name, done, count in queues:
+        q.wait_ge(sem[name], count[0])
+    g.wait_ge(sem.sent, total)

@@ -1,19 +1,23 @@
 from concourse.bass import DstId, RemoteDMATransfer
 
 N, FB, TK = 8, 64, 512
-HALF = TK // 2
+HALF, QU = TK // 2, TK // 4
+NBANK = 8
 
 SCRATCH = {
     "xs": ("sbuf", [128, TK], "float32"),
-    "ws": ("sbuf", [128, N * FB], "float32"),
+    "ws": ("sbuf", [128, 10 * FB], "float32"),
     "snd": ("sbuf", [128, N * HALF], "float32"),
     "land": ("sbuf", [128, N * HALF], "float32"),
-    "ps": ("psum", [128, 8 * TK], "float32"),
+    "ps": ("psum", [128, NBANK * TK], "float32"),
 }
-SEMAPHORES = (["ldx0", "ldx1", "ldw0", "ldw1", "ldw2", "sent", "sta", "stb"]
-              + ["mm%d" % i for i in range(8)] + ["cp%d" % i for i in range(4)] + ["arr%d" % i for i in range(N)])
+SEMAPHORES = (["sent", "sta", "stb", "own", "arx"] + ["ldx%d" % i for i in range(4)] + ["ldw%d" % i for i in range(5)]
+              + ["mm%d" % i for i in range(14)] + ["cp%d" % i for i in range(14)] + ["arr%d" % i for i in range(N)])
 
 FAR, PLANE, MATE, OWN = 0, 1, 2, 3
+SPLIT = (True, False, True, True)
+WOFF = (0, 3 * FB, 5 * FB, 8 * FB)
+WNEED = ((0,), (1, 2), (2, 3), (4,))
 
 
 def _klass(topo, a, b):
@@ -42,26 +46,24 @@ def _plan(topo, cores, j):
     groups = {}
     for r, c in enumerate(cores):
         groups.setdefault((topo.host(c), topo.chip(c)), []).append(r)
-    order = sorted(groups.values(), key=lambda gr: _klass(topo, src, cores[gr[0]]))
-    kl = [_klass(topo, src, cores[gr[0]]) for gr in order]
-    calls, away = [], 0
-    for wanted in ((FAR,), (PLANE, MATE), (OWN,)):
-        steps = [i for i in range(len(order)) if kl[i] in wanted]
-        width = max(len(order[i]) for i in steps)
-        dests = [order[i][u] for u in range(width) for i in steps if u < len(order[i]) and order[i][u] != j]
-        if not dests:
-            continue
+    by = {}
+    for gr in groups.values():
+        by[_klass(topo, src, cores[gr[0]])] = gr
+    stages = [list(by[FAR]), [by[PLANE][1], by[MATE][0]], [by[MATE][1], by[PLANE][0]], list(by[OWN])]
+    masks, away = [], 0
+    for st in stages:
+        dests = [r for r in st if r != j]
         common = topo.mask(src, cores[dests[0]])
         for r in dests:
             common &= topo.mask(src, cores[r])
-        if OWN in wanted:
+        if j in st:
             if common & ~away:
                 common &= ~away
         else:
             away |= common
         bits = _bits(common)
-        calls.append((steps, [(r, _mask(bits[n::len(dests)])) for n, r in enumerate(dests)]))
-    return order, calls
+        masks.append({r: _mask(bits[n::len(dests)]) for n, r in enumerate(dests)})
+    return stages, masks, [by[FAR], by[PLANE], by[MATE], by[PLANE], by[OWN]]
 
 
 def rank_program(g, core, T, topo):
@@ -70,83 +72,120 @@ def rank_program(g, core, T, topo):
         return
     cores = list(T.cores)
     sem = T.sem
-    order, calls = _plan(topo, cores, j)
-
-    def cols(gr):
-        return FB * gr[0], FB * (gr[-1] + 1)
-
-    lo, hi = cols(order[0])
-    ranges = [(lo, hi)] + sorted(
-        [rg for rg in ((0, lo), (hi, N * FB)) if rg[0] < rg[1]],
-        key=lambda rg: min(i for i, gr in enumerate(order) if rg[0] <= FB * gr[0] < rg[1]))
-    g.sync.dma_start(T.xs[:, 0:HALF], T.x[:, 0:HALF]).then_inc(sem.ldx0, 16)
-    g.sync.dma_start(T.xs[:, HALF:TK], T.x[:, HALF:TK]).then_inc(sem.ldx1, 16)
-    for n, (a, b) in enumerate(ranges):
-        g.scalar.dma_start(T.ws[:, a:b], T.w[:, a:b]).then_inc(sem["ldw%d" % n], 16)
-
-    seen = set()
+    stages, masks, pairs = _plan(topo, cores, j)
 
     def wait_once(q, done, name, val):
         if name not in done:
             done.add(name)
             q.wait_ge(sem[name], val)
 
-    for i, gr in enumerate(order):
-        a, b = cols(gr)
-        n = [k for k, rg in enumerate(ranges) if rg[0] <= a < rg[1]][0]
-        wait_once(g.tensor, seen, "ldw%d" % n, 16)
-        for h in (0, 1):
-            wait_once(g.tensor, seen, "ldx%d" % h, 16)
-            bank = TK * (2 * i + h)
-            g.tensor.matmul(T.ps[:, bank:bank + HALF], T.ws[:, a:b], T.xs[:, HALF * h:HALF * (h + 1)],
-                            start=True, stop=True).then_inc(sem["mm%d" % (2 * i + h)], 1)
+    def load_x(q, n):
+        q.dma_start(T.xs[:, QU * n:QU * (n + 1)], T.x[:, QU * n:QU * (n + 1)]).then_inc(sem["ldx%d" % n], 16)
 
-    for i, gr in enumerate(order):
-        for h in (0, 1):
-            g.vector.wait_ge(sem["mm%d" % (2 * i + h)], 1)
-            bank = TK * (2 * i + h)
-            p = 0 if h == j % 2 else FB
-            for u, r in enumerate(gr):
-                out = T.land[p:p + FB, HALF * j:HALF * (j + 1)] if r == j else T.snd[p:p + FB, HALF * r:HALF * (r + 1)]
-                g.vector.tensor_copy(out, T.ps[FB * u:FB * (u + 1), bank:bank + HALF]).then_inc(sem["cp%d" % i], 1)
-    copies = [2 * len(gr) for gr in order]
+    def load_w(q, n):
+        a = FB * pairs[n][0]
+        q.dma_start(T.ws[:, 2 * FB * n:2 * FB * (n + 1)], T.w[:, a:a + 2 * FB]).then_inc(sem["ldw%d" % n], 16)
+
+    load_x(g.sync, 0)
+    load_w(g.scalar, 0)
+    load_x(g.sync, 2)
+    load_x(g.scalar, 1)
+    load_x(g.sync, 3)
+    load_w(g.scalar, 1)
+    load_w(g.sync, 2)
+    load_w(g.scalar, 3)
+    load_w(g.sync, 4)
+
+    steps = []
+    for i in range(len(stages)):
+        if SPLIT[i]:
+            steps += [(i, c0, c0 + QU) for c0 in (0, HALF, QU, HALF + QU)]
+        else:
+            steps += [(i, 0, HALF), (i, HALF, TK)]
+    away = [len([r for r in stages[i] if r != j]) for i, _, _ in steps]
+
+    seen = set()
+    for idx, (i, c0, c1) in enumerate(steps):
+        for n in WNEED[i]:
+            wait_once(g.tensor, seen, "ldw%d" % n, 16)
+        for n in range(c0 // QU, (c1 - 1) // QU + 1):
+            wait_once(g.tensor, seen, "ldx%d" % n, 16)
+        if idx >= NBANK:
+            g.tensor.wait_ge(sem["cp%d" % (idx - NBANK)], away[idx - NBANK])
+        bank = TK * (idx % NBANK)
+        g.tensor.matmul(T.ps[:, bank:bank + c1 - c0], T.ws[:, WOFF[i]:WOFF[i] + 2 * FB], T.xs[:, c0:c1],
+                        start=True, stop=True).then_inc(sem["mm%d" % idx], 1)
+
+    n_own = 0
+    for idx, (i, c0, c1) in enumerate(steps):
+        g.vector.wait_ge(sem["mm%d" % idx], 1)
+        bank = TK * (idx % NBANK)
+        p = 0 if c0 // HALF == j % 2 else FB
+        c, wd = c0 % HALF, c1 - c0
+        for u, r in sorted(enumerate(stages[i]), key=lambda t: t[1] == j):
+            in_ = T.ps[FB * u:FB * (u + 1), bank:bank + wd]
+            if r == j:
+                g.vector.tensor_copy(T.land[p:p + FB, HALF * j + c:HALF * j + c + wd], in_).then_inc(sem.own, 1)
+                n_own += 1
+            else:
+                g.vector.tensor_copy(T.snd[p:p + FB, HALF * r + c:HALF * r + c + wd], in_).then_inc(sem["cp%d" % idx], 1)
 
     total = 0
-    for steps, sends in calls:
-        for i in steps:
-            g.wait_ge(sem["cp%d" % i], copies[i])
-        trs = []
-        for r, m in sends:
-            rid, pid = topo.addr(cores[r], core)
-            trs.append(RemoteDMATransfer(dst_ids=[DstId(rid=rid, pnc=pid)], dma_engine_mask=m, remote_sem=sem["arr%d" % j],
-                                         src=T.snd[:, HALF * r:HALF * (r + 1)], dst=T.land[:, HALF * j:HALF * (j + 1)]))
-            total += len(_bits(m))
-        g.remote_dma_fused(trs, local_sem=sem.sent)
+    for i, st in enumerate(stages):
+        idxs = [idx for idx, (k, _, _) in enumerate(steps) if k == i]
+        if SPLIT[i]:
+            pieces = [([idx for idx in idxs if steps[idx][1] % HALF == 0], 0, QU, "arx" if j in st else "arr%d" % j),
+                      ([idx for idx in idxs if steps[idx][1] % HALF != 0], QU, HALF, "arr%d" % j)]
+        else:
+            pieces = [(idxs, 0, HALF, "arr%d" % j)]
+        for need, c0, c1, name in pieces:
+            for idx in need:
+                g.wait_ge(sem["cp%d" % idx], away[idx])
+            trs = []
+            for r, m in masks[i].items():
+                rid, pid = topo.addr(cores[r], core)
+                trs.append(RemoteDMATransfer(dst_ids=[DstId(rid=rid, pnc=pid)], dma_engine_mask=m, remote_sem=sem[name],
+                                             src=T.snd[:, HALF * r + c0:HALF * r + c1],
+                                             dst=T.land[:, HALF * j + c0:HALF * j + c1]))
+                total += len(_bits(m))
+            g.remote_dma_fused(trs, local_sem=sem.sent)
 
-    stores = []
+    here = stages[-1]
+    runs = []
     for top in (True, False):
         run = None
         for s in range(N):
             y0 = TK * s + HALF * (s % 2 if top else 1 - s % 2)
-            if run is not None and run[2] + HALF * len(run[1]) == y0:
+            if run is not None and s not in here and run[1][-1] not in here and run[2] + HALF * len(run[1]) == y0:
                 run[1].append(s)
             else:
                 run = [0 if top else FB, [s], y0]
-                stores.append(run)
-    own_step = [i for i, gr in enumerate(order) if j in gr][0]
-    late = {FAR: 0, OWN: 1, MATE: 2, PLANE: 3}
-    stores.sort(key=lambda st: max(late[_klass(topo, cores[s], core)] for s in st[1]))
-    queues = ((g.sync, "sta", set(), [0]), (g.scalar, "stb", set(), [0]))
-    for n, (p, ss, y0) in enumerate(stores):
-        q, name, done, count = queues[n % 2]
-        for s in ss:
-            if s == j:
-                wait_once(q, done, "cp%d" % own_step, copies[own_step])
-            else:
-                m = [m for _, sends in _plan(topo, cores, s)[1] for r, m in sends if r == j][0]
-                wait_once(q, done, "arr%d" % s, len(_bits(m)))
-        q.dma_start(T.y[:, y0:y0 + HALF * len(ss)], T.land[p:p + FB, HALF * ss[0]:HALF * (ss[-1] + 1)]).then_inc(sem[name], 16)
-        count[0] += 16
-    for q, name, done, count in queues:
-        q.wait_ge(sem[name], count[0])
+                runs.append(run)
+
+    def lands(s):
+        st_s, mk_s, _ = _plan(topo, cores, s)
+        i = [i for i, st in enumerate(st_s) if j in st][0]
+        n = len(_bits(mk_s[i][j]))
+        return i, n, n * (2 if SPLIT[i] and s not in here else 1)
+
+    first, outer, mine, early, last = [], [], [], [], []
+    for p, ss, y0 in runs:
+        l0 = HALF * ss[0]
+        if ss[0] == j:
+            mine.append((p, l0, HALF, y0, [("own", n_own)]))
+        elif ss[0] in here:
+            early.append((p, l0, QU, y0, [("arx", lands(ss[0])[1])]))
+            last.append((p, l0 + QU, QU, y0 + QU, [("arr%d" % ss[0], lands(ss[0])[2])]))
+        else:
+            key = max(lands(s)[0] for s in ss)
+            (outer if key else first).append((key, (p, l0, HALF * len(ss), y0, [("arr%d" % s, lands(s)[2]) for s in ss])))
+    outer.sort(key=lambda t: t[0])
+    lists = ([t[1] for t in outer] + last[1:], [t[1] for t in first] + mine + early + last[:1])
+    queues = ((g.sync, "sta", set()), (g.scalar, "stb", set()))
+    for (q, name, done), sts in zip(queues, lists):
+        for p, l0, wd, y0, waits in sts:
+            for nm, val in waits:
+                wait_once(q, done, nm, val)
+            q.dma_start(T.y[:, y0:y0 + wd], T.land[p:p + FB, l0:l0 + wd]).then_inc(sem[name], 16)
+        q.wait_ge(sem[name], 16 * len(sts))
     g.wait_ge(sem.sent, total)

@@ -5,19 +5,24 @@ HALF, QU = TK // 2, TK // 4
 NBANK = 8
 
 SCRATCH = {
-    "xs": ("sbuf", [128, TK], "float32"),
-    "ws": ("sbuf", [128, 10 * FB], "float32"),
+    "inb": ("sbuf", [128, 17 * FB], "float32"),
+    "hin": ("sbuf", [128, 6 * FB], "float32"),
     "snd": ("sbuf", [128, N * HALF], "float32"),
     "land": ("sbuf", [128, N * HALF], "float32"),
     "ps": ("psum", [128, NBANK * TK], "float32"),
 }
-SEMAPHORES = (["sent", "sta", "stb", "own", "arx"] + ["ldx%d" % i for i in range(4)] + ["ldw%d" % i for i in range(5)]
+SEMAPHORES = (["sent", "sta", "stb", "own", "arx", "hop"] + ["ldx%d" % i for i in range(4)] + ["ldw%d" % i for i in range(5)]
               + ["mm%d" % i for i in range(14)] + ["cp%d" % i for i in range(14)] + ["arr%d" % i for i in range(N)])
 
 FAR, PLANE, MATE, OWN = 0, 1, 2, 3
 SPLIT = (True, False, True, True)
-WOFF = (0, 3 * FB, 5 * FB, 8 * FB)
+HST = 2
+WOFF = (0, 3 * FB, 5 * FB, 11 * FB)
 WNEED = ((0,), (1, 2), (2, 3), (4,))
+WDST = ((0, 2), (2, 2), (4, 2), (6, 1), (11, 2))
+XOFF = (7 * FB, 13 * FB, 9 * FB, 15 * FB)
+HOPOFF, HOPW = 5 * FB, 6 * FB
+_CACHE = {}
 
 
 def _klass(topo, a, b):
@@ -41,7 +46,13 @@ def _mask(bits):
     return m
 
 
+def _deal(bits, keys):
+    return {k: _mask(bits[n::len(keys)]) for n, k in enumerate(keys)}
+
+
 def _plan(topo, cores, j):
+    if j in _CACHE:
+        return _CACHE[j]
     src = cores[j]
     groups = {}
     for r, c in enumerate(cores):
@@ -61,18 +72,67 @@ def _plan(topo, cores, j):
                 common &= ~away
         else:
             away |= common
-        bits = _bits(common)
-        masks.append({r: _mask(bits[n::len(dests)]) for n, r in enumerate(dests)})
-    return stages, masks, [by[FAR], by[PLANE], by[MATE], by[PLANE], by[OWN]]
+        masks.append(_deal(_bits(common), dests))
+    world = (max(topo.host(c) for c in cores) + 1) * topo.CORES_PER_HOST
+    helper = [c for c in range(world) if c not in cores and topo.host(c) == topo.host(src)
+              and topo.chip(c) == topo.chip(src) and topo.die(c) == topo.die(src)
+              and all(topo.may_write(c, cores[r]) for r in stages[HST])][0]
+    hop = topo.mask(src, helper)
+    if hop & ~away:
+        hop &= ~away
+    common = topo.mask(helper, cores[stages[HST][0]])
+    for r in stages[HST]:
+        common &= topo.mask(helper, cores[r])
+    plan = {"stages": stages, "masks": masks, "pairs": [by[FAR], by[PLANE], by[MATE], by[PLANE], by[OWN]],
+            "helper": helper, "hop": hop, "hmasks": _deal(_bits(common), stages[HST])}
+    _CACHE[j] = plan
+    return plan
+
+
+def _top(j, n):
+    return 0 if n // 2 == j % 2 else FB
+
+
+def _helper(g, core, T, topo, cores, j):
+    sem = T.sem
+    plan = _plan(topo, cores, j)
+    st = plan["stages"][HST]
+    woff = WOFF[HST] - HOPOFF
+    g.tensor.wait_ge(sem.hop, len(_bits(plan["hop"])))
+    for t, n in enumerate((0, 2)):
+        xo = XOFF[n] - HOPOFF
+        g.tensor.matmul(T.ps[:, TK * t:TK * t + QU], T.hin[:, woff:woff + 2 * FB], T.hin[:, xo:xo + QU],
+                        start=True, stop=True).then_inc(sem["mm%d" % t], 1)
+    for t, n in enumerate((0, 2)):
+        g.vector.wait_ge(sem["mm%d" % t], 1)
+        p = _top(j, n)
+        for u in range(len(st)):
+            g.vector.tensor_copy(T.snd[p:p + FB, QU * u:QU * (u + 1)],
+                                 T.ps[FB * u:FB * (u + 1), TK * t:TK * t + QU]).then_inc(sem["cp%d" % t], 1)
+    for t in range(2):
+        g.wait_ge(sem["cp%d" % t], len(st))
+    trs, total = [], 0
+    for u, r in enumerate(st):
+        m = plan["hmasks"][r]
+        rid, pid = topo.addr(cores[r], core)
+        trs.append(RemoteDMATransfer(dst_ids=[DstId(rid=rid, pnc=pid)], dma_engine_mask=m, remote_sem=sem["arr%d" % j],
+                                     src=T.snd[:, QU * u:QU * (u + 1)], dst=T.land[:, HALF * j:HALF * j + QU]))
+        total += len(_bits(m))
+    g.remote_dma_fused(trs, local_sem=sem.sent)
+    g.wait_ge(sem.sent, total)
 
 
 def rank_program(g, core, T, topo):
+    cores = list(T.cores)
     j = T.rank_of(core)
     if j is None:
+        for s in range(N):
+            if _plan(topo, cores, s)["helper"] == core:
+                _helper(g, core, T, topo, cores, s)
         return
-    cores = list(T.cores)
     sem = T.sem
-    stages, masks, pairs = _plan(topo, cores, j)
+    plan = _plan(topo, cores, j)
+    stages, masks, pairs = plan["stages"], plan["masks"], plan["pairs"]
 
     def wait_once(q, done, name, val):
         if name not in done:
@@ -80,62 +140,65 @@ def rank_program(g, core, T, topo):
             q.wait_ge(sem[name], val)
 
     def load_x(q, n):
-        q.dma_start(T.xs[:, QU * n:QU * (n + 1)], T.x[:, QU * n:QU * (n + 1)]).then_inc(sem["ldx%d" % n], 16)
+        q.dma_start(T.inb[:, XOFF[n]:XOFF[n] + QU], T.x[:, QU * n:QU * (n + 1)]).then_inc(sem["ldx%d" % n], 16)
 
     def load_w(q, n):
-        a = FB * pairs[n][0]
-        q.dma_start(T.ws[:, 2 * FB * n:2 * FB * (n + 1)], T.w[:, a:a + 2 * FB]).then_inc(sem["ldw%d" % n], 16)
+        a, (d, k) = FB * pairs[n][0], WDST[n]
+        q.dma_start(T.inb[:, FB * d:FB * (d + k)], T.w[:, a:a + FB * k]).then_inc(sem["ldw%d" % n], 16)
 
     load_x(g.sync, 0)
     load_w(g.scalar, 0)
     load_x(g.sync, 2)
+    load_w(g.scalar, 2)
+    load_w(g.sync, 3)
     load_x(g.scalar, 1)
     load_x(g.sync, 3)
     load_w(g.scalar, 1)
-    load_w(g.sync, 2)
-    load_w(g.scalar, 3)
     load_w(g.sync, 4)
 
     steps = []
     for i in range(len(stages)):
-        if SPLIT[i]:
-            steps += [(i, c0, c0 + QU) for c0 in (0, HALF, QU, HALF + QU)]
-        else:
-            steps += [(i, 0, HALF), (i, HALF, TK)]
-    away = [len([r for r in stages[i] if r != j]) for i, _, _ in steps]
+        steps += [(i, n) for n in ((1, 3) if i == HST else (0, 2, 1, 3))]
+    away = [len([r for r in stages[i] if r != j]) for i, _ in steps]
 
     seen = set()
-    for idx, (i, c0, c1) in enumerate(steps):
-        for n in WNEED[i]:
-            wait_once(g.tensor, seen, "ldw%d" % n, 16)
-        for n in range(c0 // QU, (c1 - 1) // QU + 1):
-            wait_once(g.tensor, seen, "ldx%d" % n, 16)
+    for idx, (i, n) in enumerate(steps):
+        for k in WNEED[i]:
+            wait_once(g.tensor, seen, "ldw%d" % k, 16)
+        wait_once(g.tensor, seen, "ldx%d" % n, 16)
         if idx >= NBANK:
             g.tensor.wait_ge(sem["cp%d" % (idx - NBANK)], away[idx - NBANK])
         bank = TK * (idx % NBANK)
-        g.tensor.matmul(T.ps[:, bank:bank + c1 - c0], T.ws[:, WOFF[i]:WOFF[i] + 2 * FB], T.xs[:, c0:c1],
+        g.tensor.matmul(T.ps[:, bank:bank + QU], T.inb[:, WOFF[i]:WOFF[i] + 2 * FB], T.inb[:, XOFF[n]:XOFF[n] + QU],
                         start=True, stop=True).then_inc(sem["mm%d" % idx], 1)
 
     n_own = 0
-    for idx, (i, c0, c1) in enumerate(steps):
+    for idx, (i, n) in enumerate(steps):
         g.vector.wait_ge(sem["mm%d" % idx], 1)
         bank = TK * (idx % NBANK)
-        p = 0 if c0 // HALF == j % 2 else FB
-        c, wd = c0 % HALF, c1 - c0
+        p, c = _top(j, n), QU * (n % 2)
         for u, r in sorted(enumerate(stages[i]), key=lambda t: t[1] == j):
-            in_ = T.ps[FB * u:FB * (u + 1), bank:bank + wd]
+            in_ = T.ps[FB * u:FB * (u + 1), bank:bank + QU]
             if r == j:
-                g.vector.tensor_copy(T.land[p:p + FB, HALF * j + c:HALF * j + c + wd], in_).then_inc(sem.own, 1)
+                g.vector.tensor_copy(T.land[p:p + FB, HALF * j + c:HALF * j + c + QU], in_).then_inc(sem.own, 1)
                 n_own += 1
             else:
-                g.vector.tensor_copy(T.snd[p:p + FB, HALF * r + c:HALF * r + c + wd], in_).then_inc(sem["cp%d" % idx], 1)
+                g.vector.tensor_copy(T.snd[p:p + FB, HALF * r + c:HALF * r + c + QU], in_).then_inc(sem["cp%d" % idx], 1)
 
-    total = 0
+    for name in ("ldx0", "ldx2", "ldw2", "ldw3"):
+        g.wait_ge(sem[name], 16)
+    rid, pid = topo.addr(plan["helper"], core)
+    g.remote_dma_fused([RemoteDMATransfer(dst_ids=[DstId(rid=rid, pnc=pid)], dma_engine_mask=plan["hop"], remote_sem=sem.hop,
+                                          src=T.inb[:, HOPOFF:HOPOFF + HOPW], dst=T.hin[:, 0:HOPW])], local_sem=sem.sent)
+    total = len(_bits(plan["hop"]))
+
     for i, st in enumerate(stages):
-        idxs = [idx for idx, (k, _, _) in enumerate(steps) if k == i]
+        idxs = [idx for idx, (k, _) in enumerate(steps) if k == i]
         if SPLIT[i]:
-            pieces = [([idx for idx in idxs if steps[idx][1] % HALF == 0], 0, QU, "arx" if j in st else "arr%d" % j),
-                      ([idx for idx in idxs if steps[idx][1] % HALF != 0], QU, HALF, "arr%d" % j)]
+            pieces = [([idx for idx in idxs if steps[idx][1] % 2 == 0], 0, QU, "arx" if j in st else "arr%d" % j),
+                      ([idx for idx in idxs if steps[idx][1] % 2 == 1], QU, HALF, "arr%d" % j)]
+            if i == HST:
+                pieces = pieces[1:]
         else:
             pieces = [(idxs, 0, HALF, "arr%d" % j)]
         for need, c0, c1, name in pieces:
@@ -163,10 +226,12 @@ def rank_program(g, core, T, topo):
                 runs.append(run)
 
     def lands(s):
-        st_s, mk_s, _ = _plan(topo, cores, s)
-        i = [i for i, st in enumerate(st_s) if j in st][0]
-        n = len(_bits(mk_s[i][j]))
-        return i, n, n * (2 if SPLIT[i] and s not in here else 1)
+        ps = _plan(topo, cores, s)
+        i = [i for i, st in enumerate(ps["stages"]) if j in st][0]
+        n1 = len(_bits(ps["masks"][i][j]))
+        if s in here or not SPLIT[i]:
+            return i, n1, n1
+        return i, n1, n1 + (len(_bits(ps["hmasks"][j])) if i == HST else n1)
 
     first, outer, mine, early, last = [], [], [], [], []
     for p, ss, y0 in runs:

from concourse.bass import DstId, RemoteDMATransfer

N, FB, TK = 8, 64, 512
HALF, QU = TK // 2, TK // 4
NBANK = 8

SCRATCH = {
    "inb": ("sbuf", [128, 17 * FB], "float32"),
    "hin": ("sbuf", [128, 6 * FB], "float32"),
    "snd": ("sbuf", [128, N * HALF], "float32"),
    "land": ("sbuf", [128, N * HALF], "float32"),
    "ps": ("psum", [128, NBANK * TK], "float32"),
}
SEMAPHORES = (["sent", "sta", "stb", "own", "arx", "hop"] + ["ldx%d" % i for i in range(4)] + ["ldw%d" % i for i in range(5)]
              + ["mm%d" % i for i in range(14)] + ["cp%d" % i for i in range(14)] + ["arr%d" % i for i in range(N)])

FAR, PLANE, MATE, OWN = 0, 1, 2, 3
SPLIT = (True, False, True, True)
HST = 2
WOFF = (0, 3 * FB, 5 * FB, 11 * FB)
WNEED = ((0,), (1, 2), (2, 3), (4,))
WDST = ((0, 2), (2, 2), (4, 2), (6, 1), (11, 2))
XOFF = (7 * FB, 13 * FB, 9 * FB, 15 * FB)
HOPOFF, HOPW = 5 * FB, 6 * FB
_CACHE = {}


def _klass(topo, a, b):
    if topo.host(a) == topo.host(b) and topo.chip(a) == topo.chip(b):
        return OWN
    if topo.mates(a, b):
        return MATE
    if topo.same_plane(a, b):
        return PLANE
    return FAR


def _bits(mask):
    return [b for b in range(mask.bit_length()) if (mask >> b) & 1]


def _mask(bits):
    m = 0
    for b in bits:
        m |= 1 << b
    return m


def _deal(bits, keys):
    return {k: _mask(bits[n::len(keys)]) for n, k in enumerate(keys)}


def _plan(topo, cores, j):
    if j in _CACHE:
        return _CACHE[j]
    src = cores[j]
    groups = {}
    for r, c in enumerate(cores):
        groups.setdefault((topo.host(c), topo.chip(c)), []).append(r)
    by = {}
    for gr in groups.values():
        by[_klass(topo, src, cores[gr[0]])] = gr
    stages = [list(by[FAR]), [by[PLANE][1], by[MATE][0]], [by[MATE][1], by[PLANE][0]], list(by[OWN])]
    masks, away = [], 0
    for st in stages:
        dests = [r for r in st if r != j]
        common = topo.mask(src, cores[dests[0]])
        for r in dests:
            common &= topo.mask(src, cores[r])
        if j in st:
            if common & ~away:
                common &= ~away
        else:
            away |= common
        masks.append(_deal(_bits(common), dests))
    world = (max(topo.host(c) for c in cores) + 1) * topo.CORES_PER_HOST
    helper = [c for c in range(world) if c not in cores and topo.host(c) == topo.host(src)
              and topo.chip(c) == topo.chip(src) and topo.die(c) == topo.die(src)
              and all(topo.may_write(c, cores[r]) for r in stages[HST])][0]
    hop = topo.mask(src, helper)
    if hop & ~away:
        hop &= ~away
    common = topo.mask(helper, cores[stages[HST][0]])
    for r in stages[HST]:
        common &= topo.mask(helper, cores[r])
    plan = {"stages": stages, "masks": masks, "pairs": [by[FAR], by[PLANE], by[MATE], by[PLANE], by[OWN]],
            "helper": helper, "hop": hop, "hmasks": _deal(_bits(common), stages[HST])}
    _CACHE[j] = plan
    return plan


def _top(j, n):
    return 0 if n // 2 == j % 2 else FB


def _helper(g, core, T, topo, cores, j):
    sem = T.sem
    plan = _plan(topo, cores, j)
    st = plan["stages"][HST]
    woff = WOFF[HST] - HOPOFF
    g.tensor.wait_ge(sem.hop, len(_bits(plan["hop"])))
    for t, n in enumerate((0, 2)):
        xo = XOFF[n] - HOPOFF
        g.tensor.matmul(T.ps[:, TK * t:TK * t + QU], T.hin[:, woff:woff + 2 * FB], T.hin[:, xo:xo + QU],
                        start=True, stop=True).then_inc(sem["mm%d" % t], 1)
    for t, n in enumerate((0, 2)):
        g.vector.wait_ge(sem["mm%d" % t], 1)
        p = _top(j, n)
        for u in range(len(st)):
            g.vector.tensor_copy(T.snd[p:p + FB, QU * u:QU * (u + 1)],
                                 T.ps[FB * u:FB * (u + 1), TK * t:TK * t + QU]).then_inc(sem["cp%d" % t], 1)
    for t in range(2):
        g.wait_ge(sem["cp%d" % t], len(st))
    trs, total = [], 0
    for u, r in enumerate(st):
        m = plan["hmasks"][r]
        rid, pid = topo.addr(cores[r], core)
        trs.append(RemoteDMATransfer(dst_ids=[DstId(rid=rid, pnc=pid)], dma_engine_mask=m, remote_sem=sem["arr%d" % j],
                                     src=T.snd[:, QU * u:QU * (u + 1)], dst=T.land[:, HALF * j:HALF * j + QU]))
        total += len(_bits(m))
    g.remote_dma_fused(trs, local_sem=sem.sent)
    g.wait_ge(sem.sent, total)


def rank_program(g, core, T, topo):
    cores = list(T.cores)
    j = T.rank_of(core)
    if j is None:
        for s in range(N):
            if _plan(topo, cores, s)["helper"] == core:
                _helper(g, core, T, topo, cores, s)
        return
    sem = T.sem
    plan = _plan(topo, cores, j)
    stages, masks, pairs = plan["stages"], plan["masks"], plan["pairs"]

    def wait_once(q, done, name, val):
        if name not in done:
            done.add(name)
            q.wait_ge(sem[name], val)

    def load_x(q, n):
        q.dma_start(T.inb[:, XOFF[n]:XOFF[n] + QU], T.x[:, QU * n:QU * (n + 1)]).then_inc(sem["ldx%d" % n], 16)

    def load_w(q, n):
        a, (d, k) = FB * pairs[n][0], WDST[n]
        q.dma_start(T.inb[:, FB * d:FB * (d + k)], T.w[:, a:a + FB * k]).then_inc(sem["ldw%d" % n], 16)

    load_x(g.sync, 0)
    load_w(g.scalar, 0)
    load_x(g.sync, 2)
    load_w(g.scalar, 2)
    load_w(g.sync, 3)
    load_x(g.scalar, 1)
    load_x(g.sync, 3)
    load_w(g.scalar, 1)
    load_w(g.sync, 4)

    steps = []
    for i in range(len(stages)):
        steps += [(i, n) for n in ((1, 3) if i == HST else (0, 2, 1, 3))]
    away = [len([r for r in stages[i] if r != j]) for i, _ in steps]

    seen = set()
    for idx, (i, n) in enumerate(steps):
        for k in WNEED[i]:
            wait_once(g.tensor, seen, "ldw%d" % k, 16)
        wait_once(g.tensor, seen, "ldx%d" % n, 16)
        if idx >= NBANK:
            g.tensor.wait_ge(sem["cp%d" % (idx - NBANK)], away[idx - NBANK])
        bank = TK * (idx % NBANK)
        g.tensor.matmul(T.ps[:, bank:bank + QU], T.inb[:, WOFF[i]:WOFF[i] + 2 * FB], T.inb[:, XOFF[n]:XOFF[n] + QU],
                        start=True, stop=True).then_inc(sem["mm%d" % idx], 1)

    n_own = 0
    for idx, (i, n) in enumerate(steps):
        g.vector.wait_ge(sem["mm%d" % idx], 1)
        bank = TK * (idx % NBANK)
        p, c = _top(j, n), QU * (n % 2)
        for u, r in sorted(enumerate(stages[i]), key=lambda t: t[1] == j):
            in_ = T.ps[FB * u:FB * (u + 1), bank:bank + QU]
            if r == j:
                g.vector.tensor_copy(T.land[p:p + FB, HALF * j + c:HALF * j + c + QU], in_).then_inc(sem.own, 1)
                n_own += 1
            else:
                g.vector.tensor_copy(T.snd[p:p + FB, HALF * r + c:HALF * r + c + QU], in_).then_inc(sem["cp%d" % idx], 1)

    for name in ("ldx0", "ldx2", "ldw2", "ldw3"):
        g.wait_ge(sem[name], 16)
    rid, pid = topo.addr(plan["helper"], core)
    g.remote_dma_fused([RemoteDMATransfer(dst_ids=[DstId(rid=rid, pnc=pid)], dma_engine_mask=plan["hop"], remote_sem=sem.hop,
                                          src=T.inb[:, HOPOFF:HOPOFF + HOPW], dst=T.hin[:, 0:HOPW])], local_sem=sem.sent)
    total = len(_bits(plan["hop"]))

    for i, st in enumerate(stages):
        idxs = [idx for idx, (k, _) in enumerate(steps) if k == i]
        if SPLIT[i]:
            pieces = [([idx for idx in idxs if steps[idx][1] % 2 == 0], 0, QU, "arx" if j in st else "arr%d" % j),
                      ([idx for idx in idxs if steps[idx][1] % 2 == 1], QU, HALF, "arr%d" % j)]
            if i == HST:
                pieces = pieces[1:]
        else:
            pieces = [(idxs, 0, HALF, "arr%d" % j)]
        for need, c0, c1, name in pieces:
            for idx in need:
                g.wait_ge(sem["cp%d" % idx], away[idx])
            trs = []
            for r, m in masks[i].items():
                rid, pid = topo.addr(cores[r], core)
                trs.append(RemoteDMATransfer(dst_ids=[DstId(rid=rid, pnc=pid)], dma_engine_mask=m, remote_sem=sem[name],
                                             src=T.snd[:, HALF * r + c0:HALF * r + c1],
                                             dst=T.land[:, HALF * j + c0:HALF * j + c1]))
                total += len(_bits(m))
            g.remote_dma_fused(trs, local_sem=sem.sent)

    here = stages[-1]
    runs = []
    for top in (True, False):
        run = None
        for s in range(N):
            y0 = TK * s + HALF * (s % 2 if top else 1 - s % 2)
            if run is not None and s not in here and run[1][-1] not in here and run[2] + HALF * len(run[1]) == y0:
                run[1].append(s)
            else:
                run = [0 if top else FB, [s], y0]
                runs.append(run)

    def lands(s):
        ps = _plan(topo, cores, s)
        i = [i for i, st in enumerate(ps["stages"]) if j in st][0]
        n1 = len(_bits(ps["masks"][i][j]))
        if s in here or not SPLIT[i]:
            return i, n1, n1
        return i, n1, n1 + (len(_bits(ps["hmasks"][j])) if i == HST else n1)

    first, outer, mine, early, last = [], [], [], [], []
    for p, ss, y0 in runs:
        l0 = HALF * ss[0]
        if ss[0] == j:
            mine.append((p, l0, HALF, y0, [("own", n_own)]))
        elif ss[0] in here:
            early.append((p, l0, QU, y0, [("arx", lands(ss[0])[1])]))
            last.append((p, l0 + QU, QU, y0 + QU, [("arr%d" % ss[0], lands(ss[0])[2])]))
        else:
            key = max(lands(s)[0] for s in ss)
            (outer if key else first).append((key, (p, l0, HALF * len(ss), y0, [("arr%d" % s, lands(s)[2]) for s in ss])))
    outer.sort(key=lambda t: t[0])
    lists = ([t[1] for t in outer] + last[1:], [t[1] for t in first] + mine + early + last[:1])
    queues = ((g.sync, "sta", set()), (g.scalar, "stb", set()))
    for (q, name, done), sts in zip(queues, lists):
        for p, l0, wd, y0, waits in sts:
            for nm, val in waits:
                wait_once(q, done, nm, val)
            q.dma_start(T.y[:, y0:y0 + wd], T.land[p:p + FB, l0:l0 + wd]).then_inc(sem[name], 16)
        q.wait_ge(sem[name], 16 * len(sts))
    g.wait_ge(sem.sent, total)
